import numpy as np
import ml_dtypes


def mxq(x, axis, fmt="e4m3"):
    dtype, down = {"e4m3": (ml_dtypes.float8_e4m3fn, 7), "e5m2": (ml_dtypes.float8_e5m2, 14)}[fmt]
    v = np.moveaxis(np.asarray(x, np.float32).astype(ml_dtypes.bfloat16).astype(np.float64), axis, -1)
    blocks = v.reshape(v.shape[:-1] + (-1, 32))
    amax = np.abs(blocks).max(-1, keepdims=True)
    byte = np.maximum(np.where(amax > 0, np.frexp(amax)[1] - 1 + 127, 0) - down, 1)
    scale = np.exp2(byte - 127.0)
    codes = (blocks / scale).astype(np.float32).astype(dtype).astype(np.float64)
    return np.moveaxis((codes * scale).reshape(v.shape), -1, axis)


WIDE = False


def mx_kscale(k):
    if not WIDE:
        return np.ones(k)
    levels = np.array([10, -10, 5, -5, 0])
    if k % 512:
        return np.exp2(np.random.permutation(np.resize(levels, k // 32))).repeat(32)
    a = np.empty((k // 512, 16))
    for p in range(k // 512):
        a[p, :8] = np.random.permutation(np.resize(levels, 8))
        for g in range(8):
            far = levels[np.abs(levels - a[p, g]) >= 10]
            a[p, g + 8] = far[np.random.randint(len(far))]
    return np.exp2(a.ravel()).repeat(32)


BF16 = ml_dtypes.bfloat16


def bf(x):
    return np.asarray(x, np.float32).astype(BF16)


def f64(x):
    return np.asarray(x).astype(np.float64)

def planes(Y):
    n, m = Y.shape
    b = f64(bf(Y)).reshape(n // 32, 32, m)
    amax = np.abs(b).max(1)
    byte = np.clip(np.where(amax > 0, np.frexp(amax)[1] - 1 + 127 - 7, 1), 1, 254)
    codes = (b * np.exp2(127.0 - byte)[:, None, :]).reshape(n, m).astype(np.float32).astype(ml_dtypes.float8_e4m3fn).view(np.uint8)
    words = codes.reshape(n // 512, 128, 4, m).transpose(0, 1, 3, 2)
    return np.ascontiguousarray(words), np.ascontiguousarray(byte.astype(np.uint8).reshape(n // 512, 16, m))


R, G, M = 1024, 512, 4


def setup_inputs():
    s, u = mx_kscale(G), mx_kscale(R)
    return {
        "flux": bf(np.random.standard_normal((R, G)) * s[None, :] / u[:, None]),
        "scat": bf(np.random.standard_normal((M, G, G)) / np.sqrt(G) / s[None, :, None]),
        "dens": bf(np.random.uniform(0.2, 0.8, (R, M))),
        "nusf": bf(np.random.uniform(0.5, 1.5, (M, G)) / np.sqrt(G) / s[None, :]),
        "chi": bf(np.random.uniform(0.5, 1.5, G)),
        "kern": bf(np.random.standard_normal((R, R)) / np.sqrt(R) * u[None, :]),
        "sigt": bf(np.random.uniform(0.5, 1.5, (M, G))),
    }


def scattering_source(flux, scat, dens):
    a = mxq(flux, 1, "e4m3") @ mxq(scat, 1, "e4m3")
    return np.sum(dens.T[:, :, None] * a, axis=0)


def fission_rate(flux, nusf, dens):
    per_material = np.sum(flux[:, None, :] * nusf[None, :, :], axis=-1)
    return np.sum(dens * per_material, axis=1)


def core(flux, scat, dens, nusf, chi, kern, sigt):
    flux, scat, dens, nusf = f64(flux), f64(scat), f64(dens), f64(nusf)
    s = scattering_source(flux, scat, dens)
    f = fission_rate(flux, nusf, dens)
    q = s + f[:, None] * f64(chi)[None, :]
    c = mxq(f64(kern), 1, "e4m3") @ mxq(q, 0, "e4m3")
    st = np.sum(dens[:, :, None] * f64(sigt)[None, :, :], axis=1)
    return c / st


def reference(flux, scat, dens, nusf, chi, kern, sigt):
    R_out = core(flux, scat, dens, nusf, chi, kern, sigt)
    words, scales = planes(R_out)
    return R_out, words, scales

@@ -1,0 +1,338 @@
+from contextlib import ExitStack
+
+import concourse.mybir as mybir
+from concourse.masks import make_identity
+
+F32 = mybir.dt.float32
+BF16 = mybir.dt.bfloat16
+U32 = mybir.dt.uint32
+I32 = mybir.dt.int32
+U8 = mybir.dt.uint8
+FP8X4 = mybir.dt.float8_e4m3fn_x4
+ALU = mybir.AluOpType
+ACT = mybir.ActivationFunctionType
+AX = mybir.AxisListType
+
+P = 128
+R, G, M = 1024, 512, 4
+NT = 8
+H = 256
+FLOPS = 2 * R * G * G * M + 2 * R * R * G
+
+
+def tile_multigroupintegraltransportsourceiterati_x1_kernel(tc, flux, scat, dens, nusf, chi, kern, sigt, out_0, out_1, out_2):
+    nc = tc.nc
+    V, S, T, GP = nc.vector, nc.scalar, nc.tensor, nc.gpsimd
+    with ExitStack() as ctx:
+        keep = ctx.enter_context(tc.tile_pool(name="keep", bufs=1))
+        psum = ctx.enter_context(tc.psum_pool(name="psum", bufs=1))
+        ctx.enter_context(tc.manual_schedule())
+
+        def tile(name, shape, dtype):
+            return keep.tile(shape, dtype, align_bytes=64, name=name)
+
+        pad = tile("pad", [P, 2, G], BF16)
+        dens_pad = tile("dens_pad", [P, NT, P], BF16)
+        dens_sb = tile("dens_sb", [P, 2, 16], BF16)
+        nusf_t = tile("nusf_t", [P, M, 4], BF16)
+        flux_raw = tile("flux_raw", [P, 2, 4, G], BF16)
+        scat_raw = tile("scat_raw", [P, M, 4, G], BF16)
+        kern_raw = tile("kern_raw", [P, 2, 4, R], BF16)
+        id32 = tile("id32", [P, P], F32)
+        id16 = tile("id16", [P, P], BF16)
+        ones = tile("ones", [P, P], BF16)
+        dens32 = tile("dens32", [P, NT, M], F32)
+        dens_t = tile("dens_t", [P, NT, P], BF16)
+        flux_grp = tile("flux_grp", [P, NT, P, 4], BF16)
+        flux_codes = tile("flux_codes", [P, NT, P], U32)
+        flux_sc = tile("flux_sc", [P, NT, P], U8)
+        chi_b = tile("chi_b", [P, G], F32)
+        scat_grp = tile("scat_grp", [P, M, G, 4], BF16)
+        scat_codes = tile("scat_codes", [P, M, G], U32)
+        scat_sc = tile("scat_sc", [P, M, G], U8)
+        pd = tile("pd", [P, NT, M], F32)
+        f = tile("f", [P, NT], F32)
+        x = tile("x", [P, NT, G], F32)
+        fchi = tile("fchi", [P, NT, G], F32)
+        rs = tile("rs", [P, 2, G], F32)
+        sg = tile("sg", [P, 2, G], F32)
+        rst = tile("rst", [P, NT, G], F32)
+        kern_grp = tile("kern_grp", [P, 2, 2, 4, P, 4], BF16)
+        kern_codes = tile("kern_codes", [P, 2, 2, 4, P], U32)
+        kern_sc = tile("kern_sc", [P, 2, 2, 4, P], U8)
+        q_grp = tile("q_grp", [P, 2, G, 4], BF16)
+        q_codes = tile("q_codes", [P, 2, G], U32)
+        q_sc = tile("q_sc", [P, 2, G], U8)
+        res = tile("res", [P, 2, 4, G], F32)
+        r_grp = tile("r_grp", [P, 2, G, 4], BF16)
+        r_codes = tile("r_codes", [P, 2, G], U32)
+        r_sc = tile("r_sc", [P, 2, G], U8)
+
+        flux_v = flux.rearrange("(g p t) k -> g p t k", g=2, t=4)
+        kern_v = kern.rearrange("(g p t) k -> g p t k", g=2, t=4)
+        out0_v = out_0.rearrange("(g p t) n -> g p t n", g=2, t=4)
+        out1_v = out_1.rearrange("g p n t -> g p (n t)").bitcast(I32)
+        out2_v = out_2.bitcast(I32)
+
+        def mm_bank(shape):
+            return psum.tile(shape, F32, tag="mm", bufs=4, name="mm")
+
+        def tp_bank(shape, dtype=F32):
+            return psum.tile(shape, dtype, tag="tp", bufs=2, name="tp")
+
+        def load_scat(m):
+            nc.sync.dma_start(out=scat_raw[:, m], in_=scat[m].rearrange("(p j) n -> p j n", j=4))
+
+        def flux_bank(b, eng):
+            g, t0 = divmod(2 * b, 4)
+            tp = tp_bank([P, 2, 2, P])
+            for a in range(2):
+                words = flux_raw[:, g, t0 + a].bitcast(F32)
+                for u in range(2):
+                    T.transpose(tp[:, a, u], words[:, u:256:2], id32[:])
+            dst = flux_grp[:, 2 * b:2 * b + 2].rearrange("p a r f -> p a (r f)").bitcast(F32).rearrange("p a (r u) -> p a r u", u=2)
+            src = tp[:].rearrange("p a u r -> p a r u")
+            if eng == "S":
+                S.copy(out=dst, in_=src)
+            else:
+                V.tensor_copy(out=dst, in_=src)
+
+        def flux_quant(b):
+            V.quantize_mx(out=flux_codes[:, 2 * b:2 * b + 2].rearrange("p a r -> p (a r)").bitcast(FP8X4),
+                          scales=flux_sc[:, 2 * b:2 * b + 2].rearrange("p a r -> p (a r)"),
+                          in_=flux_grp[:, 2 * b:2 * b + 2].rearrange("p a r f -> p (a r f)"))
+
+        def inv_st(i):
+            st = psum.tile([P, G], F32, tag="st", bufs=1, name="st")
+            T.matmul(st[:], lhsT=dens_t[:, i], rhs=pad[:, 1], start=True, stop=True)
+            k = i % 2
+            S.activation(out=rs[:, k], in_=st[:], func=ACT.Abs_reciprocal_sqrt)
+            S.activation(out=sg[:, k], in_=st[:], func=ACT.Sign)
+            S.activation(out=rs[:, k], in_=rs[:, k], func=ACT.Square)
+            GP.tensor_tensor(out=rst[:, i], in0=rs[:, k], in1=sg[:, k], op=ALU.mult)
+
+        def scat_inter(m, eng):
+            o = scat_grp[:, m].rearrange("p (c i) t -> p c t i", i=4)
+            s = scat_raw[:, m].rearrange("p t (c i) -> p c t i", i=4)
+            if eng == "V":
+                V.tensor_copy(out=o, in_=s)
+            elif eng == "S":
+                S.copy(out=o, in_=s)
+            else:
+                GP.tensor_scalar(out=scat_grp[:, m], in0=scat_raw[:, m].rearrange("p t n -> p n t"), scalar1=1.0, scalar2=0.0, op0=ALU.mult, op1=ALU.add)
+
+        def scat_quant(m):
+            V.quantize_mx(out=scat_codes[:, m].bitcast(FP8X4), scales=scat_sc[:, m],
+                          in_=scat_grp[:, m].rearrange("p n j -> p (n j)"))
+
+        p_ps = psum.tile([P, NT, M], F32, tag="p", bufs=1, name="p_ps")
+
+        fis_left = [(i, j) for i in range(NT) for j in range(4)]
+
+        def fis(n):
+            for k in range(n):
+                i, j = fis_left.pop(0)
+                T.matmul(p_ps[:, i], lhsT=flux_grp[:, i, :, j], rhs=nusf_t[:, :, j], start=(j == 0), stop=(j == 3))
+
+        def fission1():
+            V.tensor_tensor(out=pd[:], in0=p_ps[:], in1=dens32[:], op=ALU.mult)
+
+        def fission2():
+            V.tensor_reduce(out=f[:], in_=pd[:], axis=AX.X, op=ALU.add)
+
+        def amat(i, m, c0, w):
+            a = mm_bank([P, G])
+            T.matmul_mx(out=a[:, 0:w], lhsT=flux_codes[:, i].bitcast(FP8X4), lhsT_scale=flux_sc[:, i],
+                        rhs=scat_codes[:, m, c0:c0 + w].bitcast(FP8X4), rhs_scale=scat_sc[:, m, c0:c0 + w],
+                        start=True, stop=True)
+            return a
+
+        def mix0(i):
+            a = amat(i, 0, 0, G)
+            S.activation(out=x[:, i], in_=a[:], func=ACT.Copy, scale=dens32[:, i, 0:1])
+
+        def mixf(i, c0):
+            GP.tensor_scalar(out=fchi[:, i, c0:c0 + H], in0=chi_b[:, c0:c0 + H], scalar1=f[:, i:i + 1], scalar2=0.0, op0=ALU.mult, op1=ALU.add)
+
+        def mix(i, m, c0=0, w=G):
+            a = amat(i, m, c0, w)
+            V.scalar_tensor_tensor(out=x[:, i, c0:c0 + w], in0=a[:, 0:w], scalar=dens32[:, i, m:m + 1],
+                                   in1=x[:, i, c0:c0 + w], op0=ALU.mult, op1=ALU.add)
+
+        def kern_bank(i):
+            g, t = divmod(i, 4)
+            tp = tp_bank([P, 2, 2, P])
+            words = kern_raw[:, g, t].bitcast(F32)
+            for ks in range(2):
+                for u in range(2):
+                    T.transpose(tp[:, ks, u], words[:, 256 * ks + u:256 * ks + 256:2], id32[:])
+            dst = kern_grp[:, g, :, t].rearrange("p k r f -> p k (r f)").bitcast(F32).rearrange("p k (r u) -> p k r u", u=2)
+            S.copy(out=dst, in_=tp[:].rearrange("p k u r -> p k r u"))
+
+        def kern_quant(g, ks):
+            V.quantize_mx(out=kern_codes[:, g, ks].rearrange("p t r -> p (t r)").bitcast(FP8X4),
+                          scales=kern_sc[:, g, ks].rearrange("p t r -> p (t r)"),
+                          in_=kern_grp[:, g, ks].rearrange("p t r f -> p (t r f)"))
+
+        def q_inter(g, c0, w):
+            V.tensor_tensor(out=q_grp[:, g, c0:c0 + w], in0=x[:, 4 * g:4 * g + 4, c0:c0 + w].rearrange("p t n -> p n t"),
+                            in1=fchi[:, 4 * g:4 * g + 4, c0:c0 + w].rearrange("p t n -> p n t"), op=ALU.add)
+
+        def q_quant(g, c0, w):
+            V.quantize_mx(out=q_codes[:, g, c0:c0 + w].bitcast(FP8X4), scales=q_sc[:, g, c0:c0 + w],
+                          in_=q_grp[:, g, c0:c0 + w].rearrange("p n t -> p (n t)"))
+
+        def trans_mm(g, tt, c0):
+            c = mm_bank([P, 2, H])
+            for a in range(2):
+                for gs in range(2):
+                    T.matmul_mx(out=c[:, a], lhsT=kern_codes[:, g, gs, 2 * tt + a].bitcast(FP8X4),
+                                lhsT_scale=kern_sc[:, g, gs, 2 * tt + a],
+                                rhs=q_codes[:, gs, c0:c0 + H].bitcast(FP8X4), rhs_scale=q_sc[:, gs, c0:c0 + H],
+                                start=(gs == 0), stop=(gs == 1))
+            return c
+
+        def trans_out(c, g, tt, c0):
+            i = 4 * g + 2 * tt
+            V.tensor_tensor(out=res[:, g, 2 * tt:2 * tt + 2, c0:c0 + H], in0=c[:], in1=rst[:, i:i + 2, c0:c0 + H], op=ALU.mult)
+            nc.sync.dma_start(out=out0_v[g, :, 2 * tt:2 * tt + 2, c0:c0 + H], in_=res[:, g, 2 * tt:2 * tt + 2, c0:c0 + H])
+
+        def r_inter(g, c0, w, eng):
+            o, s = r_grp[:, g, c0:c0 + w], res[:, g, :, c0:c0 + w].rearrange("p t n -> p n t")
+            if eng == "S":
+                S.copy(out=o, in_=s)
+            else:
+                V.tensor_copy(out=o, in_=s)
+
+        def r_quant(g, c0, w):
+            V.quantize_mx(out=r_codes[:, g, c0:c0 + w].bitcast(FP8X4), scales=r_sc[:, g, c0:c0 + w],
+                          in_=r_grp[:, g, c0:c0 + w].rearrange("p n t -> p (n t)"))
+            nc.sync.dma_start(out=out1_v[g, :, c0:c0 + w], in_=r_codes[:, g, c0:c0 + w].bitcast(I32))
+
+        def r_scales(g):
+            for k in range(4):
+                nc.scalar.dma_start(out=out2_v[g, 4 * k:4 * k + 4, :], in_=r_sc[32 * k:32 * k + 4, g, :].bitcast(I32))
+
+        V.memset(pad[:], 0.0)
+        GP.memset(dens_pad[:], 0.0)
+        make_identity(nc, id32[:])
+        nc.scalar.dma_start(out=dens_sb[:], in_=dens.rearrange("(g p t) m -> p g (t m)", g=2, t=4))
+        nc.scalar.dma_start(out=pad[0:4, 1, :], in_=sigt)
+        load_scat(0)
+        nc.sync.dma_start(out=flux_raw[:, 0], in_=flux_v[0])
+        load_scat(1)
+        nc.sync.dma_start(out=flux_raw[:, 1], in_=flux_v[1])
+        load_scat(2)
+        with nc.allow_non_contiguous_dma("512 short runs of nusf"):
+            nc.scalar.dma_start(out=nusf_t[:], in_=nusf.rearrange("m (p j) -> p m j", j=4))
+        nc.scalar.dma_start(out=pad[0:1, 0, :], in_=chi.unsqueeze(0))
+        load_scat(3)
+        for g in range(2):
+            nc.sync.dma_start(out=kern_raw[:, g], in_=kern_v[g])
+        V.memset(ones[:], 1.0)
+        V.tensor_copy(out=id16[:], in_=id32[:])
+        V.tensor_copy(out=dens_pad[:, :, 0:M], in_=dens_sb[:].rearrange("p g (t m) -> p (g t) m", m=M))
+        V.tensor_copy(out=dens32[:], in_=dens_sb[:].rearrange("p g (t m) -> p (g t) m", m=M))
+        dt_ps = tp_bank([P, NT, P], BF16)
+        for i in range(NT):
+            T.transpose(dt_ps[:, i], dens_pad[:, i], id16[:])
+        S.copy(out=dens_t[:], in_=dt_ps[:])
+        inv_st(0)
+        scat_inter(0, "V")
+        flux_bank(0, "V")
+        scat_quant(0)
+        flux_bank(1, "S")
+        flux_quant(0)
+        flux_bank(2, "S")
+        scat_inter(1, "V")
+        scat_inter(2, "G")
+        scat_inter(3, "G")
+        flux_quant(1)
+        flux_bank(3, "S")
+        mix0(0)
+        mix0(1)
+        flux_quant(2)
+        scat_quant(1)
+        flux_quant(3)
+        mix0(2)
+        mix(0, 1)
+        mix0(3)
+        mix(1, 1)
+        mix0(4)
+        mix(2, 1)
+        mix0(5)
+        mix(3, 1)
+        mix0(6)
+        mix(4, 1)
+        mix0(7)
+        scat_quant(2)
+        inv_st(1)
+        for i in range(5, NT):
+            fis(2)
+            mix(i, 1)
+        chi_ps = tp_bank([P, G])
+        T.matmul(chi_ps[:], lhsT=ones[:], rhs=pad[:, 0], start=True, stop=True)
+        S.copy(out=chi_b[:], in_=chi_ps[:])
+        inv_st(2)
+        for i in range(NT):
+            mix(i, 2)
+            fis(3)
+            if i == 3:
+                inv_st(3)
+                scat_quant(3)
+        fis(2)
+        inv_st(4)
+        fission1()
+        mix(0, 3, 0, H)
+        fission2()
+        for i in range(NT):
+            mixf(i, 0)
+        for i in range(NT):
+            mixf(i, H)
+        for i in range(1, NT):
+            mix(i, 3, 0, H)
+            if i % 2:
+                kern_bank((i - 1) // 2)
+            if i == 6:
+                q_inter(0, 0, H)
+                inv_st(5)
+        for i in range(4, 8):
+            kern_bank(i)
+        q_inter(1, 0, H)
+        q_quant(0, 0, H)
+        kern_quant(0, 0)
+        kern_quant(0, 1)
+        q_quant(1, 0, H)
+        for i in range(0, NT):
+            mix(i, 3, H, H)
+            if i == 3:
+                kern_quant(1, 0)
+                kern_quant(1, 1)
+            if i == 5:
+                q_inter(0, H, H)
+                inv_st(6)
+            if i == 6:
+                q_quant(0, H, H)
+        inv_st(7)
+        cs = [trans_mm(0, 0, 0)]
+        cs.append(trans_mm(0, 1, 0))
+        q_inter(1, H, H)
+        trans_out(cs[0], 0, 0, 0)
+        q_quant(1, H, H)
+        trans_out(cs[1], 0, 1, 0)
+        r_inter(0, 0, H, "S")
+        todo = [(1, 0, 0), (1, 1, 0), (0, 0, H), (0, 1, H), (1, 0, H), (1, 1, H)]
+        for k, a in enumerate(todo):
+            c = trans_mm(*a)
+            trans_out(c, *a)
+            if k == 1:
+                r_inter(1, 0, H, "S")
+                r_quant(0, 0, H)
+            if k == 3:
+                r_inter(0, H, H, "S")
+                r_quant(1, 0, H)
+        r_inter(1, H, H, "V")
+        r_quant(0, H, H)
+        r_quant(1, H, H)
+        r_scales(0)
+        r_scales(1)

@@ -102,14 +102,18 @@ def tile_multigroupintegraltransportsourceiterati_x1_kernel(tc, flux, scat, dens
                           scales=flux_sc[:, 2 * b:2 * b + 2].rearrange("p a r -> p (a r)"),
                           in_=flux_grp[:, 2 * b:2 * b + 2].rearrange("p a r f -> p (a r f)"))
 
-        def inv_st(i):
-            st = psum.tile([P, G], F32, tag="st", bufs=1, name="st")
-            T.matmul(st[:], lhsT=dens_t[:, i], rhs=pad[:, 1], start=True, stop=True)
-            k = i % 2
-            S.activation(out=rs[:, k], in_=st[:], func=ACT.Abs_reciprocal_sqrt)
-            S.activation(out=sg[:, k], in_=st[:], func=ACT.Sign)
-            S.activation(out=rs[:, k], in_=rs[:, k], func=ACT.Square)
-            GP.tensor_tensor(out=rst[:, i], in0=rs[:, k], in1=sg[:, k], op=ALU.mult)
+        def inv_st(i, parts="ab"):
+            if "a" in parts:
+                st = psum.tile([P, G], F32, tag="st", bufs=1, name="st")
+                T.matmul(st[:], lhsT=dens_t[:, i], rhs=pad[:, 1], start=True, stop=True)
+                S.activation(out=rs[:, i % 2], in_=st[:], func=ACT.Abs_reciprocal_sqrt)
+                S.activation(out=sg[:, i % 2], in_=st[:], func=ACT.Sign)
+            if "b" in parts:
+                S.activation(out=rs[:, i % 2], in_=rs[:, i % 2], func=ACT.Square)
+                for c0 in (0, H):
+                    (V if i in VSIGN else GP).tensor_tensor(out=rst[:, i, c0:c0 + H], in0=rs[:, i % 2, c0:c0 + H], in1=sg[:, i % 2, c0:c0 + H], op=ALU.mult)
+
+        VSIGN = ()
 
         def scat_inter(m, eng):
             o = scat_grp[:, m].rearrange("p (c i) t -> p c t i", i=4)
@@ -119,7 +123,9 @@ def tile_multigroupintegraltransportsourceiterati_x1_kernel(tc, flux, scat, dens
             elif eng == "S":
                 S.copy(out=o, in_=s)
             else:
-                GP.tensor_scalar(out=scat_grp[:, m], in0=scat_raw[:, m].rearrange("p t n -> p n t"), scalar1=1.0, scalar2=0.0, op0=ALU.mult, op1=ALU.add)
+                for c0 in range(0, G, P):
+                    GP.tensor_scalar(out=scat_grp[:, m, c0:c0 + P], in0=scat_raw[:, m, :, c0:c0 + P].rearrange("p t n -> p n t"),
+                                     scalar1=1.0, scalar2=0.0, op0=ALU.mult, op1=ALU.add)
 
         def scat_quant(m):
             V.quantize_mx(out=scat_codes[:, m].bitcast(FP8X4), scales=scat_sc[:, m],
@@ -134,11 +140,11 @@ def tile_multigroupintegraltransportsourceiterati_x1_kernel(tc, flux, scat, dens
                 i, j = fis_left.pop(0)
                 T.matmul(p_ps[:, i], lhsT=flux_grp[:, i, :, j], rhs=nusf_t[:, :, j], start=(j == 0), stop=(j == 3))
 
-        def fission1():
-            V.tensor_tensor(out=pd[:], in0=p_ps[:], in1=dens32[:], op=ALU.mult)
+        def fission1(g):
+            V.tensor_tensor(out=pd[:, 4 * g:4 * g + 4], in0=p_ps[:, 4 * g:4 * g + 4], in1=dens32[:, 4 * g:4 * g + 4], op=ALU.mult)
 
-        def fission2():
-            V.tensor_reduce(out=f[:], in_=pd[:], axis=AX.X, op=ALU.add)
+        def fission2(g):
+            V.tensor_reduce(out=f[:, 4 * g:4 * g + 4], in_=pd[:, 4 * g:4 * g + 4], axis=AX.X, op=ALU.add)
 
         def amat(i, m, c0, w):
             a = mm_bank([P, G])
@@ -151,8 +157,11 @@ def tile_multigroupintegraltransportsourceiterati_x1_kernel(tc, flux, scat, dens
             a = amat(i, 0, 0, G)
             S.activation(out=x[:, i], in_=a[:], func=ACT.Copy, scale=dens32[:, i, 0:1])
 
-        def mixf(i, c0):
-            GP.tensor_scalar(out=fchi[:, i, c0:c0 + H], in0=chi_b[:, c0:c0 + H], scalar1=f[:, i:i + 1], scalar2=0.0, op0=ALU.mult, op1=ALU.add)
+        def mixf(i, eng):
+            if eng == "S":
+                S.activation(out=fchi[:, i], in_=chi_b[:], func=ACT.Copy, scale=f[:, i:i + 1])
+            else:
+                GP.tensor_scalar(out=fchi[:, i], in0=chi_b[:], scalar1=f[:, i:i + 1], scalar2=0.0, op0=ALU.mult, op1=ALU.add)
 
         def mix(i, m, c0=0, w=G):
             a = amat(i, m, c0, w)
@@ -175,8 +184,10 @@ def tile_multigroupintegraltransportsourceiterati_x1_kernel(tc, flux, scat, dens
                           in_=kern_grp[:, g, ks].rearrange("p t r f -> p (t r f)"))
 
         def q_inter(g, c0, w):
-            V.tensor_tensor(out=q_grp[:, g, c0:c0 + w], in0=x[:, 4 * g:4 * g + 4, c0:c0 + w].rearrange("p t n -> p n t"),
-                            in1=fchi[:, 4 * g:4 * g + 4, c0:c0 + w].rearrange("p t n -> p n t"), op=ALU.add)
+            t4 = slice(4 * g, 4 * g + 4)
+            V.tensor_tensor(out=q_grp[:, g, c0:c0 + w].rearrange("p (c i) t -> p c t i", i=4),
+                            in0=x[:, t4, c0:c0 + w].rearrange("p t (c i) -> p c t i", i=4),
+                            in1=fchi[:, t4, c0:c0 + w].rearrange("p t (c i) -> p c t i", i=4), op=ALU.add)
 
         def q_quant(g, c0, w):
             V.quantize_mx(out=q_codes[:, g, c0:c0 + w].bitcast(FP8X4), scales=q_sc[:, g, c0:c0 + w],
@@ -198,7 +209,8 @@ def tile_multigroupintegraltransportsourceiterati_x1_kernel(tc, flux, scat, dens
             nc.sync.dma_start(out=out0_v[g, :, 2 * tt:2 * tt + 2, c0:c0 + H], in_=res[:, g, 2 * tt:2 * tt + 2, c0:c0 + H])
 
         def r_inter(g, c0, w, eng):
-            o, s = r_grp[:, g, c0:c0 + w], res[:, g, :, c0:c0 + w].rearrange("p t n -> p n t")
+            o = r_grp[:, g, c0:c0 + w].rearrange("p (c i) t -> p c t i", i=4)
+            s = res[:, g, :, c0:c0 + w].rearrange("p t (c i) -> p c t i", i=4)
             if eng == "S":
                 S.copy(out=o, in_=s)
             else:
@@ -237,16 +249,15 @@ def tile_multigroupintegraltransportsourceiterati_x1_kernel(tc, flux, scat, dens
         for i in range(NT):
             T.transpose(dt_ps[:, i], dens_pad[:, i], id16[:])
         S.copy(out=dens_t[:], in_=dt_ps[:])
-        inv_st(0)
         scat_inter(0, "V")
+        inv_st(0)
         flux_bank(0, "V")
         scat_quant(0)
         flux_bank(1, "S")
         flux_quant(0)
+        inv_st(1, "a")
         flux_bank(2, "S")
         scat_inter(1, "V")
-        scat_inter(2, "G")
-        scat_inter(3, "G")
         flux_quant(1)
         flux_bank(3, "S")
         mix0(0)
@@ -254,6 +265,8 @@ def tile_multigroupintegraltransportsourceiterati_x1_kernel(tc, flux, scat, dens
         flux_quant(2)
         scat_quant(1)
         flux_quant(3)
+        inv_st(1, "b")
+        scat_inter(2, "G")
         mix0(2)
         mix(0, 1)
         mix0(3)
@@ -262,73 +275,73 @@ def tile_multigroupintegraltransportsourceiterati_x1_kernel(tc, flux, scat, dens
         mix(2, 1)
         mix0(5)
         mix(3, 1)
+        scat_inter(3, "V")
+        fis(2)
         mix0(6)
         mix(4, 1)
+        fis(4)
         mix0(7)
-        scat_quant(2)
-        inv_st(1)
+        inv_st(2)
         for i in range(5, NT):
-            fis(2)
             mix(i, 1)
+            fis(4 if i == 5 else 2)
+        scat_quant(2)
         chi_ps = tp_bank([P, G])
         T.matmul(chi_ps[:], lhsT=ones[:], rhs=pad[:, 0], start=True, stop=True)
         S.copy(out=chi_b[:], in_=chi_ps[:])
-        inv_st(2)
+        inv_st(3)
         for i in range(NT):
             mix(i, 2)
-            fis(3)
+            if i == 1:
+                fission1(0)
+            if i == 2:
+                fission2(0)
+            fis((2, 2, 2, 2, 2, 2, 3, 3)[i])
             if i == 3:
-                inv_st(3)
                 scat_quant(3)
-        fis(2)
-        inv_st(4)
-        fission1()
-        mix(0, 3, 0, H)
-        fission2()
-        for i in range(NT):
-            mixf(i, 0)
-        for i in range(NT):
-            mixf(i, H)
-        for i in range(1, NT):
-            mix(i, 3, 0, H)
-            if i % 2:
-                kern_bank((i - 1) // 2)
-            if i == 6:
-                q_inter(0, 0, H)
-                inv_st(5)
-        for i in range(4, 8):
+                mixf(0, "S")
+                mixf(1, "S")
+                inv_st(4)
+        mixf(2, "S")
+        mixf(3, "S")
+        for i in range(4):
+            mix(i, 3)
             kern_bank(i)
-        q_inter(1, 0, H)
-        q_quant(0, 0, H)
+            if i == 1:
+                fission1(1)
+            if i == 2:
+                fission2(1)
+                for j in range(4):
+                    mixf(4 + j, "G")
+        q_inter(0, 0, G)
+        kern_bank(4)
+        mix(4, 3)
+        inv_st(5)
         kern_quant(0, 0)
+        q_quant(0, 0, G)
         kern_quant(0, 1)
+        for i in range(5, 8):
+            kern_bank(i)
+            mix(i, 3)
+        inv_st(6)
+        q_inter(1, 0, H)
+        kern_quant(1, 0)
         q_quant(1, 0, H)
-        for i in range(0, NT):
-            mix(i, 3, H, H)
-            if i == 3:
-                kern_quant(1, 0)
-                kern_quant(1, 1)
-            if i == 5:
-                q_inter(0, H, H)
-                inv_st(6)
-            if i == 6:
-                q_quant(0, H, H)
-        inv_st(7)
-        cs = [trans_mm(0, 0, 0)]
-        cs.append(trans_mm(0, 1, 0))
         q_inter(1, H, H)
-        trans_out(cs[0], 0, 0, 0)
-        q_quant(1, H, H)
-        trans_out(cs[1], 0, 1, 0)
-        r_inter(0, 0, H, "S")
-        todo = [(1, 0, 0), (1, 1, 0), (0, 0, H), (0, 1, H), (1, 0, H), (1, 1, H)]
+        kern_quant(1, 1)
+        inv_st(7)
+        todo = [(0, 0, 0), (0, 1, 0), (1, 0, 0), (1, 1, 0), (0, 0, H), (0, 1, H), (1, 0, H), (1, 1, H)]
         for k, a in enumerate(todo):
             c = trans_mm(*a)
             trans_out(c, *a)
+            if k == 0:
+                q_quant(1, H, H)
             if k == 1:
+                r_inter(0, 0, H, "S")
+            if k == 3:
                 r_inter(1, 0, H, "S")
                 r_quant(0, 0, H)
-            if k == 3:
+            if k == 5:
                 r_inter(0, H, H, "S")
                 r_quant(1, 0, H)
         r_inter(1, H, H, "V")

@@ -31,7 +31,8 @@ def tile_multigroupintegraltransportsourceiterati_x1_kernel(tc, flux, scat, dens
         def tile(name, shape, dtype):
             return keep.tile(shape, dtype, align_bytes=64, name=name)
 
-        pad = tile("pad", [P, 2, G], BF16)
+        sig4 = tile("sig4", [M, G], BF16)
+        pad = tile("pad", [P, G], BF16)
         dens_pad = tile("dens_pad", [P, NT, P], BF16)
         dens_sb = tile("dens_sb", [P, 2, 16], BF16)
         nusf_t = tile("nusf_t", [P, M, 4], BF16)
@@ -40,22 +41,21 @@ def tile_multigroupintegraltransportsourceiterati_x1_kernel(tc, flux, scat, dens
         kern_raw = tile("kern_raw", [P, 2, 4, R], BF16)
         id32 = tile("id32", [P, P], F32)
         id16 = tile("id16", [P, P], BF16)
-        ones = tile("ones", [P, P], BF16)
         dens32 = tile("dens32", [P, NT, M], F32)
         dens_t = tile("dens_t", [P, NT, P], BF16)
         flux_grp = tile("flux_grp", [P, NT, P, 4], BF16)
         flux_codes = tile("flux_codes", [P, NT, P], U32)
         flux_sc = tile("flux_sc", [P, NT, P], U8)
-        chi_b = tile("chi_b", [P, G], F32)
+        chi_b = tile("chi_b", [P, G], BF16)
         scat_grp = tile("scat_grp", [P, M, G, 4], BF16)
         scat_codes = tile("scat_codes", [P, M, G], U32)
         scat_sc = tile("scat_sc", [P, M, G], U8)
         pd = tile("pd", [P, NT, M], F32)
         f = tile("f", [P, NT], F32)
         x = tile("x", [P, NT, G], F32)
-        fchi = tile("fchi", [P, NT, G], F32)
-        rs = tile("rs", [P, 2, G], F32)
-        sg = tile("sg", [P, 2, G], F32)
+        fchi_t = tile("fchi_t", [P, NT, G], F32)
+        rs = tile("rs", [P, 3, G], F32)
+        sg = tile("sg", [P, 3, G], F32)
         rst = tile("rst", [P, NT, G], F32)
         kern_grp = tile("kern_grp", [P, 2, 2, 4, P, 4], BF16)
         kern_codes = tile("kern_codes", [P, 2, 2, 4, P], U32)
@@ -68,11 +68,14 @@ def tile_multigroupintegraltransportsourceiterati_x1_kernel(tc, flux, scat, dens
         r_codes = tile("r_codes", [P, 2, G], U32)
         r_sc = tile("r_sc", [P, 2, G], U8)
 
+        dens_v = dens_sb[:].rearrange("p g (t m) -> p (g t) m", m=M)
         flux_v = flux.rearrange("(g p t) k -> g p t k", g=2, t=4)
         kern_v = kern.rearrange("(g p t) k -> g p t k", g=2, t=4)
         out0_v = out_0.rearrange("(g p t) n -> g p t n", g=2, t=4)
         out1_v = out_1.rearrange("g p n t -> g p (n t)").bitcast(I32)
         out2_v = out_2.bitcast(I32)
+
+        bank = {}
 
         def mm_bank(shape):
             return psum.tile(shape, F32, tag="mm", bufs=4, name="mm")
@@ -80,272 +83,389 @@ def tile_multigroupintegraltransportsourceiterati_x1_kernel(tc, flux, scat, dens
         def tp_bank(shape, dtype=F32):
             return psum.tile(shape, dtype, tag="tp", bufs=2, name="tp")
 
-        def load_scat(m):
-            nc.sync.dma_start(out=scat_raw[:, m], in_=scat[m].rearrange("(p j) n -> p j n", j=4))
+        p_ps = psum.tile([P, NT, M], F32, tag="p", bufs=1, name="p_ps")
 
-        def flux_bank(b, eng):
-            g, t0 = divmod(2 * b, 4)
-            tp = tp_bank([P, 2, 2, P])
-            for a in range(2):
-                words = flux_raw[:, g, t0 + a].bitcast(F32)
-                for u in range(2):
-                    T.transpose(tp[:, a, u], words[:, u:256:2], id32[:])
-            dst = flux_grp[:, 2 * b:2 * b + 2].rearrange("p a r f -> p a (r f)").bitcast(F32).rearrange("p a (r u) -> p a r u", u=2)
-            src = tp[:].rearrange("p a u r -> p a r u")
+        def move(eng, out, in_):
             if eng == "S":
-                S.copy(out=dst, in_=src)
+                S.copy(out=out, in_=in_)
             else:
-                V.tensor_copy(out=dst, in_=src)
+                V.tensor_copy(out=out, in_=in_)
 
-        def flux_quant(b):
+        def t_dens():
+            bank["dens"] = tp_bank([P, NT, P], BF16)
+            for i in range(NT):
+                T.transpose(bank["dens"][:, i], dens_pad[:, i], id16[:])
+
+        def t_flux(b):
+            bank["flux", b] = tp_bank([P, 2, 2, P])
+            for a in range(2):
+                words = flux_raw[:, b // 2, 2 * (b % 2) + a].bitcast(F32)
+                for u in range(2):
+                    T.transpose(bank["flux", b][:, a, u], words[:, u:256:2], id32[:])
+
+        def t_kern(i):
+            bank["kern", i] = tp_bank([P, 2, 2, P])
+            words = kern_raw[:, i // 4, i % 4].bitcast(F32)
+            for ks in range(2):
+                for u in range(2):
+                    T.transpose(bank["kern", i][:, ks, u], words[:, 256 * ks + u:256 * ks + 256:2], id32[:])
+
+        def st(i):
+            bank["st", i] = psum.tile([P, G], F32, tag="st", bufs=1, name="st")
+            T.matmul(bank["st", i][:], lhsT=dens_t[:, i], rhs=pad[:], start=True, stop=True)
+
+        def mx(i, m):
+            bank["a", i, m] = mm_bank([P, G])
+            T.matmul_mx(out=bank["a", i, m][:], lhsT=flux_codes[:, i].bitcast(FP8X4), lhsT_scale=flux_sc[:, i],
+                        rhs=scat_codes[:, m].bitcast(FP8X4), rhs_scale=scat_sc[:, m], start=True, stop=True)
+
+        def fis(i):
+            for j in range(4):
+                T.matmul(p_ps[:, i], lhsT=flux_grp[:, i, :, j], rhs=nusf_t[:, :, j], start=(j == 0), stop=(j == 3))
+
+        def tr(g, c0):
+            bank["c", g, c0] = mm_bank([P, 4, P])
+            for t in range(4):
+                for gs in range(2):
+                    T.matmul_mx(out=bank["c", g, c0][:, t], lhsT=kern_codes[:, g, gs, t].bitcast(FP8X4),
+                                lhsT_scale=kern_sc[:, g, gs, t], rhs=q_codes[:, gs, c0:c0 + P].bitcast(FP8X4),
+                                rhs_scale=q_sc[:, gs, c0:c0 + P], start=(gs == 0), stop=(gs == 1))
+
+        def c_dens():
+            S.copy(out=dens_t[:], in_=bank["dens"][:])
+
+        def c_pad():
+            S.copy(out=pad[0:M], in_=sig4[:])
+
+        def c_flux(b, eng):
+            dst = flux_grp[:, 2 * b:2 * b + 2].rearrange("p a r f -> p a (r f)").bitcast(F32).rearrange("p a (r u) -> p a r u", u=2)
+            move(eng, dst, bank["flux", b][:].rearrange("p a u r -> p a r u"))
+
+        def c_kern(i, eng):
+            dst = kern_grp[:, i // 4, :, i % 4].rearrange("p k r f -> p k (r f)").bitcast(F32).rearrange("p k (r u) -> p k r u", u=2)
+            move(eng, dst, bank["kern", i][:].rearrange("p k u r -> p k r u"))
+
+        def x0(i, eng):
+            if eng == "S":
+                S.activation(out=x[:, i], in_=bank["a", i, 0][:], func=ACT.Copy, scale=dens32[:, i, 0:1])
+            else:
+                V.tensor_scalar(out=x[:, i], in0=bank["a", i, 0][:], scalar1=dens32[:, i, 0:1], scalar2=None, op0=ALU.mult)
+
+        def ars(i):
+            S.activation(out=rs[:, i % 3], in_=bank["st", i][:], func=ACT.Abs_reciprocal_sqrt)
+
+        def sgn(i):
+            S.activation(out=sg[:, i % 3], in_=bank["st", i][:], func=ACT.Sign)
+
+        def sqr(i):
+            S.activation(out=rs[:, i % 3], in_=rs[:, i % 3], func=ACT.Square)
+
+        def fchi(i, eng):
+            if eng == "S":
+                S.activation(out=fchi_t[:, i], in_=chi_b[:], func=ACT.Copy, scale=f[:, i:i + 1])
+            else:
+                (V if eng == "V" else GP).tensor_scalar(out=fchi_t[:, i], in0=chi_b[:], scalar1=f[:, i:i + 1], scalar2=0.0, op0=ALU.mult, op1=ALU.add)
+
+        def inv(i):
+            ars(i)
+            sgn(i)
+            sqr(i)
+
+        def r_int(g, c0, w, eng):
+            move(eng, r_grp[:, g, c0:c0 + w].rearrange("p (c i) t -> p c t i", i=4),
+                 res[:, g, :, c0:c0 + w].rearrange("p t (c i) -> p c t i", i=4))
+
+        def s_piece(m, c0, eng):
+            if eng == "V":
+                V.tensor_copy(out=scat_grp[:, m, c0:c0 + H].rearrange("p (c i) t -> p c t i", i=4),
+                              in_=scat_raw[:, m, :, c0:c0 + H].rearrange("p t (c i) -> p c t i", i=4))
+            elif eng == "S":
+                S.copy(out=scat_grp[:, m, c0:c0 + H].rearrange("p (c i) t -> p c t i", i=4),
+                       in_=scat_raw[:, m, :, c0:c0 + H].rearrange("p t (c i) -> p c t i", i=4))
+            else:
+                for b0 in (c0, c0 + P):
+                    GP.tensor_scalar(out=scat_grp[:, m, b0:b0 + P], in0=scat_raw[:, m, :, b0:b0 + P].rearrange("p t n -> p n t"),
+                                     scalar1=1.0, scalar2=0.0, op0=ALU.mult, op1=ALU.add)
+
+        def rmul(i, eng):
+            if eng == "V":
+                V.tensor_tensor(out=rst[:, i], in0=rs[:, i % 3], in1=sg[:, i % 3], op=ALU.mult)
+            else:
+                for c0 in (0, H):
+                    GP.tensor_tensor(out=rst[:, i, c0:c0 + H], in0=rs[:, i % 3, c0:c0 + H], in1=sg[:, i % 3, c0:c0 + H], op=ALU.mult)
+
+        def s_int(m):
+            V.tensor_copy(out=scat_grp[:, m].rearrange("p (c i) t -> p c t i", i=4),
+                          in_=scat_raw[:, m].rearrange("p t (c i) -> p c t i", i=4))
+
+        def q_scat(m):
+            V.quantize_mx(out=scat_codes[:, m].bitcast(FP8X4), scales=scat_sc[:, m], in_=scat_grp[:, m].rearrange("p n j -> p (n j)"))
+
+        def q_flux(b):
             V.quantize_mx(out=flux_codes[:, 2 * b:2 * b + 2].rearrange("p a r -> p (a r)").bitcast(FP8X4),
                           scales=flux_sc[:, 2 * b:2 * b + 2].rearrange("p a r -> p (a r)"),
                           in_=flux_grp[:, 2 * b:2 * b + 2].rearrange("p a r f -> p (a r f)"))
 
-        def inv_st(i, parts="ab"):
-            if "a" in parts:
-                st = psum.tile([P, G], F32, tag="st", bufs=1, name="st")
-                T.matmul(st[:], lhsT=dens_t[:, i], rhs=pad[:, 1], start=True, stop=True)
-                S.activation(out=rs[:, i % 2], in_=st[:], func=ACT.Abs_reciprocal_sqrt)
-                S.activation(out=sg[:, i % 2], in_=st[:], func=ACT.Sign)
-            if "b" in parts:
-                S.activation(out=rs[:, i % 2], in_=rs[:, i % 2], func=ACT.Square)
-                for c0 in (0, H):
-                    (V if i in VSIGN else GP).tensor_tensor(out=rst[:, i, c0:c0 + H], in0=rs[:, i % 2, c0:c0 + H], in1=sg[:, i % 2, c0:c0 + H], op=ALU.mult)
+        def q_kern(g, ks):
+            V.quantize_mx(out=kern_codes[:, g, ks].rearrange("p t r -> p (t r)").bitcast(FP8X4),
+                          scales=kern_sc[:, g, ks].rearrange("p t r -> p (t r)"), in_=kern_grp[:, g, ks].rearrange("p t r f -> p (t r f)"))
 
-        VSIGN = ()
+        def stt(i, m):
+            V.scalar_tensor_tensor(out=x[:, i], in0=bank["a", i, m][:], scalar=dens32[:, i, m:m + 1], in1=x[:, i], op0=ALU.mult, op1=ALU.add)
 
-        def scat_inter(m, eng):
-            o = scat_grp[:, m].rearrange("p (c i) t -> p c t i", i=4)
-            s = scat_raw[:, m].rearrange("p t (c i) -> p c t i", i=4)
-            if eng == "V":
-                V.tensor_copy(out=o, in_=s)
-            elif eng == "S":
-                S.copy(out=o, in_=s)
-            else:
-                for c0 in range(0, G, P):
-                    GP.tensor_scalar(out=scat_grp[:, m, c0:c0 + P], in0=scat_raw[:, m, :, c0:c0 + P].rearrange("p t n -> p n t"),
-                                     scalar1=1.0, scalar2=0.0, op0=ALU.mult, op1=ALU.add)
-
-        def scat_quant(m):
-            V.quantize_mx(out=scat_codes[:, m].bitcast(FP8X4), scales=scat_sc[:, m],
-                          in_=scat_grp[:, m].rearrange("p n j -> p (n j)"))
-
-        p_ps = psum.tile([P, NT, M], F32, tag="p", bufs=1, name="p_ps")
-
-        fis_left = [(i, j) for i in range(NT) for j in range(4)]
-
-        def fis(n):
-            for k in range(n):
-                i, j = fis_left.pop(0)
-                T.matmul(p_ps[:, i], lhsT=flux_grp[:, i, :, j], rhs=nusf_t[:, :, j], start=(j == 0), stop=(j == 3))
-
-        def fission1(g):
+        def f_mul(g):
             V.tensor_tensor(out=pd[:, 4 * g:4 * g + 4], in0=p_ps[:, 4 * g:4 * g + 4], in1=dens32[:, 4 * g:4 * g + 4], op=ALU.mult)
 
-        def fission2(g):
+        def f_sum(g):
             V.tensor_reduce(out=f[:, 4 * g:4 * g + 4], in_=pd[:, 4 * g:4 * g + 4], axis=AX.X, op=ALU.add)
 
-        def amat(i, m, c0, w):
-            a = mm_bank([P, G])
-            T.matmul_mx(out=a[:, 0:w], lhsT=flux_codes[:, i].bitcast(FP8X4), lhsT_scale=flux_sc[:, i],
-                        rhs=scat_codes[:, m, c0:c0 + w].bitcast(FP8X4), rhs_scale=scat_sc[:, m, c0:c0 + w],
-                        start=True, stop=True)
-            return a
-
-        def mix0(i):
-            a = amat(i, 0, 0, G)
-            S.activation(out=x[:, i], in_=a[:], func=ACT.Copy, scale=dens32[:, i, 0:1])
-
-        def mixf(i, eng):
-            if eng == "S":
-                S.activation(out=fchi[:, i], in_=chi_b[:], func=ACT.Copy, scale=f[:, i:i + 1])
-            else:
-                GP.tensor_scalar(out=fchi[:, i], in0=chi_b[:], scalar1=f[:, i:i + 1], scalar2=0.0, op0=ALU.mult, op1=ALU.add)
-
-        def mix(i, m, c0=0, w=G):
-            a = amat(i, m, c0, w)
-            V.scalar_tensor_tensor(out=x[:, i, c0:c0 + w], in0=a[:, 0:w], scalar=dens32[:, i, m:m + 1],
-                                   in1=x[:, i, c0:c0 + w], op0=ALU.mult, op1=ALU.add)
-
-        def kern_bank(i):
-            g, t = divmod(i, 4)
-            tp = tp_bank([P, 2, 2, P])
-            words = kern_raw[:, g, t].bitcast(F32)
-            for ks in range(2):
-                for u in range(2):
-                    T.transpose(tp[:, ks, u], words[:, 256 * ks + u:256 * ks + 256:2], id32[:])
-            dst = kern_grp[:, g, :, t].rearrange("p k r f -> p k (r f)").bitcast(F32).rearrange("p k (r u) -> p k r u", u=2)
-            S.copy(out=dst, in_=tp[:].rearrange("p k u r -> p k r u"))
-
-        def kern_quant(g, ks):
-            V.quantize_mx(out=kern_codes[:, g, ks].rearrange("p t r -> p (t r)").bitcast(FP8X4),
-                          scales=kern_sc[:, g, ks].rearrange("p t r -> p (t r)"),
-                          in_=kern_grp[:, g, ks].rearrange("p t r f -> p (t r f)"))
-
-        def q_inter(g, c0, w):
+        def q_int(g, c0, w):
             t4 = slice(4 * g, 4 * g + 4)
             V.tensor_tensor(out=q_grp[:, g, c0:c0 + w].rearrange("p (c i) t -> p c t i", i=4),
                             in0=x[:, t4, c0:c0 + w].rearrange("p t (c i) -> p c t i", i=4),
-                            in1=fchi[:, t4, c0:c0 + w].rearrange("p t (c i) -> p c t i", i=4), op=ALU.add)
+                            in1=fchi_t[:, t4, c0:c0 + w].rearrange("p t (c i) -> p c t i", i=4), op=ALU.add)
 
-        def q_quant(g, c0, w):
+        def q_q(g, c0, w):
             V.quantize_mx(out=q_codes[:, g, c0:c0 + w].bitcast(FP8X4), scales=q_sc[:, g, c0:c0 + w],
                           in_=q_grp[:, g, c0:c0 + w].rearrange("p n t -> p (n t)"))
 
-        def trans_mm(g, tt, c0):
-            c = mm_bank([P, 2, H])
-            for a in range(2):
-                for gs in range(2):
-                    T.matmul_mx(out=c[:, a], lhsT=kern_codes[:, g, gs, 2 * tt + a].bitcast(FP8X4),
-                                lhsT_scale=kern_sc[:, g, gs, 2 * tt + a],
-                                rhs=q_codes[:, gs, c0:c0 + H].bitcast(FP8X4), rhs_scale=q_sc[:, gs, c0:c0 + H],
-                                start=(gs == 0), stop=(gs == 1))
-            return c
+        def out(g, c0):
+            V.tensor_tensor(out=res[:, g, :, c0:c0 + P], in0=bank["c", g, c0][:], in1=rst[:, 4 * g:4 * g + 4, c0:c0 + P], op=ALU.mult)
 
-        def trans_out(c, g, tt, c0):
-            i = 4 * g + 2 * tt
-            V.tensor_tensor(out=res[:, g, 2 * tt:2 * tt + 2, c0:c0 + H], in0=c[:], in1=rst[:, i:i + 2, c0:c0 + H], op=ALU.mult)
-            nc.sync.dma_start(out=out0_v[g, :, 2 * tt:2 * tt + 2, c0:c0 + H], in_=res[:, g, 2 * tt:2 * tt + 2, c0:c0 + H])
-
-        def r_inter(g, c0, w, eng):
-            o = r_grp[:, g, c0:c0 + w].rearrange("p (c i) t -> p c t i", i=4)
-            s = res[:, g, :, c0:c0 + w].rearrange("p t (c i) -> p c t i", i=4)
-            if eng == "S":
-                S.copy(out=o, in_=s)
-            else:
-                V.tensor_copy(out=o, in_=s)
-
-        def r_quant(g, c0, w):
+        def q_r(g, c0, w):
             V.quantize_mx(out=r_codes[:, g, c0:c0 + w].bitcast(FP8X4), scales=r_sc[:, g, c0:c0 + w],
                           in_=r_grp[:, g, c0:c0 + w].rearrange("p n t -> p (n t)"))
+
+        def v_pad():
+            V.memset(pad[:], 0.0)
+
+        def v_id():
+            V.tensor_copy(out=id16[:], in_=id32[:])
+
+        def v_dens():
+            V.tensor_copy(out=dens_pad[:, :, 0:M], in_=dens_v)
+
+        def v_dens32():
+            V.tensor_copy(out=dens32[:], in_=dens_v)
+
+        warm = tile("warm", [P, 2], F32)
+
+        def v_warm():
+            V.memset(warm[:], 1.0)
+
+        def s_warm():
+            S.activation(out=warm[:, 1:2], in_=warm[:, 0:1], func=ACT.Abs_reciprocal_sqrt)
+
+        def store(g, c0, w):
+            nc.sync.dma_start(out=out0_v[g, :, :, c0:c0 + w], in_=res[:, g, :, c0:c0 + w])
+
+        def store_w(g, c0, w):
             nc.sync.dma_start(out=out1_v[g, :, c0:c0 + w], in_=r_codes[:, g, c0:c0 + w].bitcast(I32))
 
-        def r_scales(g):
-            for k in range(4):
-                nc.scalar.dma_start(out=out2_v[g, 4 * k:4 * k + 4, :], in_=r_sc[32 * k:32 * k + 4, g, :].bitcast(I32))
+        def store_s(g, k, eng):
+            (nc.scalar if eng == "S" else nc.sync).dma_start(out=out2_v[g, 4 * k:4 * k + 4, :], in_=r_sc[32 * k:32 * k + 4, g, :].bitcast(I32))
 
-        V.memset(pad[:], 0.0)
-        GP.memset(dens_pad[:], 0.0)
-        make_identity(nc, id32[:])
-        nc.scalar.dma_start(out=dens_sb[:], in_=dens.rearrange("(g p t) m -> p g (t m)", g=2, t=4))
-        nc.scalar.dma_start(out=pad[0:4, 1, :], in_=sigt)
-        load_scat(0)
-        nc.sync.dma_start(out=flux_raw[:, 0], in_=flux_v[0])
-        load_scat(1)
-        nc.sync.dma_start(out=flux_raw[:, 1], in_=flux_v[1])
-        load_scat(2)
-        with nc.allow_non_contiguous_dma("512 short runs of nusf"):
-            nc.scalar.dma_start(out=nusf_t[:], in_=nusf.rearrange("m (p j) -> p m j", j=4))
-        nc.scalar.dma_start(out=pad[0:1, 0, :], in_=chi.unsqueeze(0))
-        load_scat(3)
-        for g in range(2):
+        def load_scat(m):
+            nc.sync.dma_start(out=scat_raw[:, m], in_=scat[m].rearrange("(p j) n -> p j n", j=4))
+
+        def load_flux(g):
+            nc.sync.dma_start(out=flux_raw[:, g], in_=flux_v[g])
+
+        def load_kern(g):
             nc.sync.dma_start(out=kern_raw[:, g], in_=kern_v[g])
-        V.memset(ones[:], 1.0)
-        V.tensor_copy(out=id16[:], in_=id32[:])
-        V.tensor_copy(out=dens_pad[:, :, 0:M], in_=dens_sb[:].rearrange("p g (t m) -> p (g t) m", m=M))
-        V.tensor_copy(out=dens32[:], in_=dens_sb[:].rearrange("p g (t m) -> p (g t) m", m=M))
-        dt_ps = tp_bank([P, NT, P], BF16)
-        for i in range(NT):
-            T.transpose(dt_ps[:, i], dens_pad[:, i], id16[:])
-        S.copy(out=dens_t[:], in_=dt_ps[:])
-        scat_inter(0, "V")
-        inv_st(0)
-        flux_bank(0, "V")
-        scat_quant(0)
-        flux_bank(1, "S")
-        flux_quant(0)
-        inv_st(1, "a")
-        flux_bank(2, "S")
-        scat_inter(1, "V")
-        flux_quant(1)
-        flux_bank(3, "S")
-        mix0(0)
-        mix0(1)
-        flux_quant(2)
-        scat_quant(1)
-        flux_quant(3)
-        inv_st(1, "b")
-        scat_inter(2, "G")
-        mix0(2)
-        mix(0, 1)
-        mix0(3)
-        mix(1, 1)
-        mix0(4)
-        mix(2, 1)
-        mix0(5)
-        mix(3, 1)
-        scat_inter(3, "V")
-        fis(2)
-        mix0(6)
-        mix(4, 1)
-        fis(4)
-        mix0(7)
-        inv_st(2)
-        for i in range(5, NT):
-            mix(i, 1)
-            fis(4 if i == 5 else 2)
-        scat_quant(2)
-        chi_ps = tp_bank([P, G])
-        T.matmul(chi_ps[:], lhsT=ones[:], rhs=pad[:, 0], start=True, stop=True)
-        S.copy(out=chi_b[:], in_=chi_ps[:])
-        inv_st(3)
-        for i in range(NT):
-            mix(i, 2)
-            if i == 1:
-                fission1(0)
-            if i == 2:
-                fission2(0)
-            fis((2, 2, 2, 2, 2, 2, 3, 3)[i])
-            if i == 3:
-                scat_quant(3)
-                mixf(0, "S")
-                mixf(1, "S")
-                inv_st(4)
-        mixf(2, "S")
-        mixf(3, "S")
-        for i in range(4):
-            mix(i, 3)
-            kern_bank(i)
-            if i == 1:
-                fission1(1)
-            if i == 2:
-                fission2(1)
-                for j in range(4):
-                    mixf(4 + j, "G")
-        q_inter(0, 0, G)
-        kern_bank(4)
-        mix(4, 3)
-        inv_st(5)
-        kern_quant(0, 0)
-        q_quant(0, 0, G)
-        kern_quant(0, 1)
-        for i in range(5, 8):
-            kern_bank(i)
-            mix(i, 3)
-        inv_st(6)
-        q_inter(1, 0, H)
-        kern_quant(1, 0)
-        q_quant(1, 0, H)
-        q_inter(1, H, H)
-        kern_quant(1, 1)
-        inv_st(7)
-        todo = [(0, 0, 0), (0, 1, 0), (1, 0, 0), (1, 1, 0), (0, 0, H), (0, 1, H), (1, 0, H), (1, 1, H)]
-        for k, a in enumerate(todo):
-            c = trans_mm(*a)
-            trans_out(c, *a)
-            if k == 0:
-                q_quant(1, H, H)
+
+        def load_small():
+            nc.scalar.dma_start(out=dens_sb[:], in_=dens.rearrange("(g p t) m -> p g (t m)", g=2, t=4))
+            nc.scalar.dma_start(out=sig4[:], in_=sigt)
+            with nc.allow_non_contiguous_dma("512 short runs of nusf"):
+                nc.scalar.dma_start(out=nusf_t[:], in_=nusf.rearrange("m (p j) -> p m j", j=4))
+
+        def load_chi():
+            nc.sync.dma_start(out=chi_b[:], in_=chi.partition_broadcast(P))
+
+        def g_start():
+            GP.memset(dens_pad[:], 0.0)
+            make_identity(nc, id32[:])
+
+        load_small()
+        load_flux(0)
+        load_scat(0)
+        load_flux(1)
+        load_scat(1)
+        load_scat(2)
+        load_scat(3)
+        load_chi()
+        load_kern(0)
+        load_kern(1)
+        g_start()
+        v_warm()
+        s_warm()
+        v_pad()
+        v_id()
+        v_dens()
+        v_dens32()
+        t_dens()
+        c_dens()
+        c_pad()
+        s_int(0)
+        for b in range(2):
+            t_flux(b)
+            c_flux(b, "S")
+        st(0)
+        inv(0)
+        q_flux(0)
+        q_scat(0)
+        for b in range(2, 4):
+            t_flux(b)
+            c_flux(b, "S")
+        s_int(1)
+        q_flux(1)
+        q_scat(1)
+        s_piece(2, 0, "G")
+        s_piece(2, H, "V")
+        s_piece(3, H, "G")
+        q_flux(2)
+        q_flux(3)
+        s_piece(3, 0, "V")
+        rmul(0, "G")
+        mx(0, 0)
+        x0(0, "S")
+        st(1)
+        ars(1)
+        sgn(1)
+        fis(0)
+        mx(1, 0)
+        x0(1, "S")
+        mx(2, 0)
+        x0(2, "S")
+        for k in range(5):
+            mx(k, 1)
+            stt(k, 1)
             if k == 1:
-                r_inter(0, 0, H, "S")
-            if k == 3:
-                r_inter(1, 0, H, "S")
-                r_quant(0, 0, H)
+                st(2)
+            mx(k + 3, 0)
+            x0(k + 3, "S")
+            if k == 0:
+                fis(1)
+        sqr(1)
+        rmul(1, "G")
+        inv(2)
+        rmul(2, "G")
+        mx(5, 1)
+        stt(5, 1)
+        t_kern(0)
+        q_scat(2)
+        q_scat(3)
+        for k in (6, 7):
+            mx(k, 1)
+            stt(k, 1)
+        fis(2)
+        fis(3)
+        mx(0, 2)
+        stt(0, 2)
+        f_mul(0)
+        st(3)
+        ars(3)
+        sgn(3)
+        c_kern(0, "S")
+        sqr(3)
+        rmul(3, "G")
+        mx(1, 2)
+        stt(1, 2)
+        f_sum(0)
+        for k in (2, 3):
+            mx(k, 2)
+            stt(k, 2)
+        fchi(0, "G")
+        fchi(1, "G")
+        mx(0, 3)
+        stt(0, 3)
+        fis(4)
+        st(4)
+        inv(4)
+        rmul(4, "G")
+        for k in (1, 2):
+            mx(k, 3)
+            stt(k, 3)
+        t_kern(1)
+        c_kern(1, "S")
+        mx(3, 3)
+        stt(3, 3)
+        for k in range(4, 8):
+            mx(k, 2)
+            stt(k, 2)
             if k == 5:
-                r_inter(0, H, H, "S")
-                r_quant(1, 0, H)
-        r_inter(1, H, H, "V")
-        r_quant(0, H, H)
-        r_quant(1, H, H)
-        r_scales(0)
-        r_scales(1)
+                st(5)
+                ars(5)
+                fis(5)
+        fchi(2, "S")
+        fchi(3, "S")
+        sgn(5)
+        sqr(5)
+        rmul(5, "G")
+        fis(6)
+        fis(7)
+        f_mul(1)
+        mx(4, 3)
+        stt(4, 3)
+        f_sum(1)
+        q_int(0, 0, H)
+        q_int(0, H, H)
+        for k in range(5, 8):
+            mx(k, 3)
+            stt(k, 3)
+        fchi(4, "S")
+        st(6)
+        for i in range(2, 6):
+            t_kern(i)
+            c_kern(i, "S")
+            if i == 2:
+                fchi(5, "S")
+                fchi(6, "S")
+            if i == 4:
+                fchi(7, "S")
+        inv(6)
+        for i in range(6, 8):
+            t_kern(i)
+            c_kern(i, "S")
+        st(7)
+        inv(7)
+        rmul(7, "G")
+        q_kern(0, 0)
+        q_kern(0, 1)
+        q_int(1, 0, H)
+        q_q(0, 0, G)
+        q_q(1, 0, H)
+        q_int(1, H, H)
+        rmul(6, "V")
+        q_q(1, H, H)
+        q_kern(1, 0)
+        q_kern(1, 1)
+        for g, c0 in ((0, 0), (1, 0), (0, H)):
+            for b0 in (c0, c0 + P):
+                tr(g, b0)
+                out(g, b0)
+            store(g, c0, H)
+            r_int(g, c0, H, "S")
+        tr(1, H)
+        out(1, H)
+        store(1, H, P)
+        q_r(0, 0, H)
+        store_w(0, 0, H)
+        tr(1, H + P)
+        out(1, H + P)
+        store(1, H + P, P)
+        r_int(1, H, P, "S")
+        q_r(1, 0, H)
+        store_w(1, 0, H)
+        r_int(1, H + P, P, "V")
+        q_r(0, H, H)
+        store_w(0, H, H)
+        q_r(1, H, P)
+        q_r(1, H + P, P)
+        for k in range(4):
+            store_s(0, k, "S")
+        store_w(1, H, P)
+        store_w(1, H + P, P)
+        for k in range(4):
+            store_s(1, k, "S" if k % 2 else "Y")

from contextlib import ExitStack

import concourse.mybir as mybir
from concourse.masks import make_identity

F32 = mybir.dt.float32
BF16 = mybir.dt.bfloat16
U32 = mybir.dt.uint32
I32 = mybir.dt.int32
U8 = mybir.dt.uint8
FP8X4 = mybir.dt.float8_e4m3fn_x4
ALU = mybir.AluOpType
ACT = mybir.ActivationFunctionType
AX = mybir.AxisListType

P = 128
R, G, M = 1024, 512, 4
NT = 8
H = 256
FLOPS = 2 * R * G * G * M + 2 * R * R * G


def tile_multigroupintegraltransportsourceiterati_x1_kernel(tc, flux, scat, dens, nusf, chi, kern, sigt, out_0, out_1, out_2):
    nc = tc.nc
    V, S, T, GP = nc.vector, nc.scalar, nc.tensor, nc.gpsimd
    with ExitStack() as ctx:
        keep = ctx.enter_context(tc.tile_pool(name="keep", bufs=1))
        psum = ctx.enter_context(tc.psum_pool(name="psum", bufs=1))
        ctx.enter_context(tc.manual_schedule())

        def tile(name, shape, dtype):
            return keep.tile(shape, dtype, align_bytes=64, name=name)

        sig4 = tile("sig4", [M, G], BF16)
        pad = tile("pad", [P, G], BF16)
        dens_pad = tile("dens_pad", [P, NT, P], BF16)
        dens_sb = tile("dens_sb", [P, 2, 16], BF16)
        nusf_t = tile("nusf_t", [P, M, 4], BF16)
        flux_raw = tile("flux_raw", [P, 2, 4, G], BF16)
        scat_raw = tile("scat_raw", [P, M, 4, G], BF16)
        kern_raw = tile("kern_raw", [P, 2, 4, R], BF16)
        id32 = tile("id32", [P, P], F32)
        id16 = tile("id16", [P, P], BF16)
        dens32 = tile("dens32", [P, NT, M], F32)
        dens_t = tile("dens_t", [P, NT, P], BF16)
        flux_grp = tile("flux_grp", [P, NT, P, 4], BF16)
        flux_codes = tile("flux_codes", [P, NT, P], U32)
        flux_sc = tile("flux_sc", [P, NT, P], U8)
        chi_b = tile("chi_b", [P, G], BF16)
        scat_grp = tile("scat_grp", [P, M, G, 4], BF16)
        scat_codes = tile("scat_codes", [P, M, G], U32)
        scat_sc = tile("scat_sc", [P, M, G], U8)
        pd = tile("pd", [P, NT, M], F32)
        f = tile("f", [P, NT], F32)
        x = tile("x", [P, NT, G], F32)
        fchi_t = tile("fchi_t", [P, NT, G], F32)
        rs = tile("rs", [P, 3, G], F32)
        sg = tile("sg", [P, 3, G], F32)
        rst = tile("rst", [P, NT, G], F32)
        kern_grp = tile("kern_grp", [P, 2, 2, 4, P, 4], BF16)
        kern_codes = tile("kern_codes", [P, 2, 2, 4, P], U32)
        kern_sc = tile("kern_sc", [P, 2, 2, 4, P], U8)
        q_grp = tile("q_grp", [P, 2, G, 4], BF16)
        q_codes = tile("q_codes", [P, 2, G], U32)
        q_sc = tile("q_sc", [P, 2, G], U8)
        res = tile("res", [P, 2, 4, G], F32)
        r_grp = tile("r_grp", [P, 2, G, 4], BF16)
        r_codes = tile("r_codes", [P, 2, G], U32)
        r_sc = tile("r_sc", [P, 2, G], U8)

        dens_v = dens_sb[:].rearrange("p g (t m) -> p (g t) m", m=M)
        flux_v = flux.rearrange("(g p t) k -> g p t k", g=2, t=4)
        kern_v = kern.rearrange("(g p t) k -> g p t k", g=2, t=4)
        out0_v = out_0.rearrange("(g p t) n -> g p t n", g=2, t=4)
        out1_v = out_1.rearrange("g p n t -> g p (n t)").bitcast(I32)
        out2_v = out_2.bitcast(I32)

        bank = {}

        def mm_bank(shape):
            return psum.tile(shape, F32, tag="mm", bufs=4, name="mm")

        def tp_bank(shape, dtype=F32):
            return psum.tile(shape, dtype, tag="tp", bufs=2, name="tp")

        p_ps = psum.tile([P, NT, M], F32, tag="p", bufs=1, name="p_ps")

        def move(eng, out, in_):
            if eng == "S":
                S.copy(out=out, in_=in_)
            else:
                V.tensor_copy(out=out, in_=in_)

        def t_dens():
            bank["dens"] = tp_bank([P, NT, P], BF16)
            for i in range(NT):
                T.transpose(bank["dens"][:, i], dens_pad[:, i], id16[:])

        def t_flux(b):
            bank["flux", b] = tp_bank([P, 2, 2, P])
            for a in range(2):
                words = flux_raw[:, b // 2, 2 * (b % 2) + a].bitcast(F32)
                for u in range(2):
                    T.transpose(bank["flux", b][:, a, u], words[:, u:256:2], id32[:])

        def t_kern(i):
            bank["kern", i] = tp_bank([P, 2, 2, P])
            words = kern_raw[:, i // 4, i % 4].bitcast(F32)
            for ks in range(2):
                for u in range(2):
                    T.transpose(bank["kern", i][:, ks, u], words[:, 256 * ks + u:256 * ks + 256:2], id32[:])

        def st(i):
            bank["st", i] = psum.tile([P, G], F32, tag="st", bufs=1, name="st")
            T.matmul(bank["st", i][:], lhsT=dens_t[:, i], rhs=pad[:], start=True, stop=True)

        def mx(i, m):
            bank["a", i, m] = mm_bank([P, G])
            T.matmul_mx(out=bank["a", i, m][:], lhsT=flux_codes[:, i].bitcast(FP8X4), lhsT_scale=flux_sc[:, i],
                        rhs=scat_codes[:, m].bitcast(FP8X4), rhs_scale=scat_sc[:, m], start=True, stop=True)

        def fis(i):
            for j in range(4):
                T.matmul(p_ps[:, i], lhsT=flux_grp[:, i, :, j], rhs=nusf_t[:, :, j], start=(j == 0), stop=(j == 3))

        def tr(g, c0):
            bank["c", g, c0] = mm_bank([P, 4, P])
            for t in range(4):
                for gs in range(2):
                    T.matmul_mx(out=bank["c", g, c0][:, t], lhsT=kern_codes[:, g, gs, t].bitcast(FP8X4),
                                lhsT_scale=kern_sc[:, g, gs, t], rhs=q_codes[:, gs, c0:c0 + P].bitcast(FP8X4),
                                rhs_scale=q_sc[:, gs, c0:c0 + P], start=(gs == 0), stop=(gs == 1))

        def c_dens():
            S.copy(out=dens_t[:], in_=bank["dens"][:])

        def c_pad():
            S.copy(out=pad[0:M], in_=sig4[:])

        def c_flux(b, eng):
            dst = flux_grp[:, 2 * b:2 * b + 2].rearrange("p a r f -> p a (r f)").bitcast(F32).rearrange("p a (r u) -> p a r u", u=2)
            move(eng, dst, bank["flux", b][:].rearrange("p a u r -> p a r u"))

        def c_kern(i, eng):
            dst = kern_grp[:, i // 4, :, i % 4].rearrange("p k r f -> p k (r f)").bitcast(F32).rearrange("p k (r u) -> p k r u", u=2)
            move(eng, dst, bank["kern", i][:].rearrange("p k u r -> p k r u"))

        def x0(i, eng):
            if eng == "S":
                S.activation(out=x[:, i], in_=bank["a", i, 0][:], func=ACT.Copy, scale=dens32[:, i, 0:1])
            else:
                V.tensor_scalar(out=x[:, i], in0=bank["a", i, 0][:], scalar1=dens32[:, i, 0:1], scalar2=None, op0=ALU.mult)

        def ars(i):
            S.activation(out=rs[:, i % 3], in_=bank["st", i][:], func=ACT.Abs_reciprocal_sqrt)

        def sgn(i):
            S.activation(out=sg[:, i % 3], in_=bank["st", i][:], func=ACT.Sign)

        def sqr(i):
            S.activation(out=rs[:, i % 3], in_=rs[:, i % 3], func=ACT.Square)

        def fchi(i, eng):
            if eng == "S":
                S.activation(out=fchi_t[:, i], in_=chi_b[:], func=ACT.Copy, scale=f[:, i:i + 1])
            else:
                (V if eng == "V" else GP).tensor_scalar(out=fchi_t[:, i], in0=chi_b[:], scalar1=f[:, i:i + 1], scalar2=0.0, op0=ALU.mult, op1=ALU.add)

        def inv(i):
            ars(i)
            sgn(i)
            sqr(i)

        def r_int(g, c0, w, eng):
            move(eng, r_grp[:, g, c0:c0 + w].rearrange("p (c i) t -> p c t i", i=4),
                 res[:, g, :, c0:c0 + w].rearrange("p t (c i) -> p c t i", i=4))

        def s_piece(m, c0, eng):
            if eng == "V":
                V.tensor_copy(out=scat_grp[:, m, c0:c0 + H].rearrange("p (c i) t -> p c t i", i=4),
                              in_=scat_raw[:, m, :, c0:c0 + H].rearrange("p t (c i) -> p c t i", i=4))
            elif eng == "S":
                S.copy(out=scat_grp[:, m, c0:c0 + H].rearrange("p (c i) t -> p c t i", i=4),
                       in_=scat_raw[:, m, :, c0:c0 + H].rearrange("p t (c i) -> p c t i", i=4))
            else:
                for b0 in (c0, c0 + P):
                    GP.tensor_scalar(out=scat_grp[:, m, b0:b0 + P], in0=scat_raw[:, m, :, b0:b0 + P].rearrange("p t n -> p n t"),
                                     scalar1=1.0, scalar2=0.0, op0=ALU.mult, op1=ALU.add)

        def rmul(i, eng):
            if eng == "V":
                V.tensor_tensor(out=rst[:, i], in0=rs[:, i % 3], in1=sg[:, i % 3], op=ALU.mult)
            else:
                for c0 in (0, H):
                    GP.tensor_tensor(out=rst[:, i, c0:c0 + H], in0=rs[:, i % 3, c0:c0 + H], in1=sg[:, i % 3, c0:c0 + H], op=ALU.mult)

        def s_int(m):
            V.tensor_copy(out=scat_grp[:, m].rearrange("p (c i) t -> p c t i", i=4),
                          in_=scat_raw[:, m].rearrange("p t (c i) -> p c t i", i=4))

        def q_scat(m):
            V.quantize_mx(out=scat_codes[:, m].bitcast(FP8X4), scales=scat_sc[:, m], in_=scat_grp[:, m].rearrange("p n j -> p (n j)"))

        def q_flux(b):
            V.quantize_mx(out=flux_codes[:, 2 * b:2 * b + 2].rearrange("p a r -> p (a r)").bitcast(FP8X4),
                          scales=flux_sc[:, 2 * b:2 * b + 2].rearrange("p a r -> p (a r)"),
                          in_=flux_grp[:, 2 * b:2 * b + 2].rearrange("p a r f -> p (a r f)"))

        def q_kern(g, ks):
            V.quantize_mx(out=kern_codes[:, g, ks].rearrange("p t r -> p (t r)").bitcast(FP8X4),
                          scales=kern_sc[:, g, ks].rearrange("p t r -> p (t r)"), in_=kern_grp[:, g, ks].rearrange("p t r f -> p (t r f)"))

        def stt(i, m):
            V.scalar_tensor_tensor(out=x[:, i], in0=bank["a", i, m][:], scalar=dens32[:, i, m:m + 1], in1=x[:, i], op0=ALU.mult, op1=ALU.add)

        def f_mul(g):
            V.tensor_tensor(out=pd[:, 4 * g:4 * g + 4], in0=p_ps[:, 4 * g:4 * g + 4], in1=dens32[:, 4 * g:4 * g + 4], op=ALU.mult)

        def f_sum(g):
            V.tensor_reduce(out=f[:, 4 * g:4 * g + 4], in_=pd[:, 4 * g:4 * g + 4], axis=AX.X, op=ALU.add)

        def q_int(g, c0, w):
            t4 = slice(4 * g, 4 * g + 4)
            V.tensor_tensor(out=q_grp[:, g, c0:c0 + w].rearrange("p (c i) t -> p c t i", i=4),
                            in0=x[:, t4, c0:c0 + w].rearrange("p t (c i) -> p c t i", i=4),
                            in1=fchi_t[:, t4, c0:c0 + w].rearrange("p t (c i) -> p c t i", i=4), op=ALU.add)

        def q_q(g, c0, w):
            V.quantize_mx(out=q_codes[:, g, c0:c0 + w].bitcast(FP8X4), scales=q_sc[:, g, c0:c0 + w],
                          in_=q_grp[:, g, c0:c0 + w].rearrange("p n t -> p (n t)"))

        def out(g, c0):
            V.tensor_tensor(out=res[:, g, :, c0:c0 + P], in0=bank["c", g, c0][:], in1=rst[:, 4 * g:4 * g + 4, c0:c0 + P], op=ALU.mult)

        def q_r(g, c0, w):
            V.quantize_mx(out=r_codes[:, g, c0:c0 + w].bitcast(FP8X4), scales=r_sc[:, g, c0:c0 + w],
                          in_=r_grp[:, g, c0:c0 + w].rearrange("p n t -> p (n t)"))

        def v_pad():
            V.memset(pad[:], 0.0)

        def v_id():
            V.tensor_copy(out=id16[:], in_=id32[:])

        def v_dens():
            V.tensor_copy(out=dens_pad[:, :, 0:M], in_=dens_v)

        def v_dens32():
            V.tensor_copy(out=dens32[:], in_=dens_v)

        warm = tile("warm", [P, 2], F32)

        def v_warm():
            V.memset(warm[:], 1.0)

        def s_warm():
            S.activation(out=warm[:, 1:2], in_=warm[:, 0:1], func=ACT.Abs_reciprocal_sqrt)

        def store(g, c0, w):
            nc.sync.dma_start(out=out0_v[g, :, :, c0:c0 + w], in_=res[:, g, :, c0:c0 + w])

        def store_w(g, c0, w):
            nc.sync.dma_start(out=out1_v[g, :, c0:c0 + w], in_=r_codes[:, g, c0:c0 + w].bitcast(I32))

        def store_s(g, k, eng):
            (nc.scalar if eng == "S" else nc.sync).dma_start(out=out2_v[g, 4 * k:4 * k + 4, :], in_=r_sc[32 * k:32 * k + 4, g, :].bitcast(I32))

        def load_scat(m):
            nc.sync.dma_start(out=scat_raw[:, m], in_=scat[m].rearrange("(p j) n -> p j n", j=4))

        def load_flux(g):
            nc.sync.dma_start(out=flux_raw[:, g], in_=flux_v[g])

        def load_kern(g):
            nc.sync.dma_start(out=kern_raw[:, g], in_=kern_v[g])

        def load_small():
            nc.scalar.dma_start(out=dens_sb[:], in_=dens.rearrange("(g p t) m -> p g (t m)", g=2, t=4))
            nc.scalar.dma_start(out=sig4[:], in_=sigt)
            with nc.allow_non_contiguous_dma("512 short runs of nusf"):
                nc.scalar.dma_start(out=nusf_t[:], in_=nusf.rearrange("m (p j) -> p m j", j=4))

        def load_chi():
            nc.sync.dma_start(out=chi_b[:], in_=chi.partition_broadcast(P))

        def g_start():
            GP.memset(dens_pad[:], 0.0)
            make_identity(nc, id32[:])

        load_small()
        load_flux(0)
        load_scat(0)
        load_flux(1)
        load_scat(1)
        load_scat(2)
        load_scat(3)
        load_chi()
        load_kern(0)
        load_kern(1)
        g_start()
        v_warm()
        s_warm()
        v_pad()
        v_id()
        v_dens()
        v_dens32()
        t_dens()
        c_dens()
        c_pad()
        s_int(0)
        for b in range(2):
            t_flux(b)
            c_flux(b, "S")
        st(0)
        inv(0)
        q_flux(0)
        q_scat(0)
        for b in range(2, 4):
            t_flux(b)
            c_flux(b, "S")
        s_int(1)
        q_flux(1)
        q_scat(1)
        s_piece(2, 0, "G")
        s_piece(2, H, "V")
        s_piece(3, H, "G")
        q_flux(2)
        q_flux(3)
        s_piece(3, 0, "V")
        rmul(0, "G")
        mx(0, 0)
        x0(0, "S")
        st(1)
        ars(1)
        sgn(1)
        fis(0)
        mx(1, 0)
        x0(1, "S")
        mx(2, 0)
        x0(2, "S")
        for k in range(5):
            mx(k, 1)
            stt(k, 1)
            if k == 1:
                st(2)
            mx(k + 3, 0)
            x0(k + 3, "S")
            if k == 0:
                fis(1)
        sqr(1)
        rmul(1, "G")
        inv(2)
        rmul(2, "G")
        mx(5, 1)
        stt(5, 1)
        t_kern(0)
        q_scat(2)
        q_scat(3)
        for k in (6, 7):
            mx(k, 1)
            stt(k, 1)
        fis(2)
        fis(3)
        mx(0, 2)
        stt(0, 2)
        f_mul(0)
        st(3)
        ars(3)
        sgn(3)
        c_kern(0, "S")
        sqr(3)
        rmul(3, "G")
        mx(1, 2)
        stt(1, 2)
        f_sum(0)
        for k in (2, 3):
            mx(k, 2)
            stt(k, 2)
        fchi(0, "G")
        fchi(1, "G")
        mx(0, 3)
        stt(0, 3)
        fis(4)
        st(4)
        inv(4)
        rmul(4, "G")
        for k in (1, 2):
            mx(k, 3)
            stt(k, 3)
        t_kern(1)
        c_kern(1, "S")
        mx(3, 3)
        stt(3, 3)
        for k in range(4, 8):
            mx(k, 2)
            stt(k, 2)
            if k == 5:
                st(5)
                ars(5)
                fis(5)
        fchi(2, "S")
        fchi(3, "S")
        sgn(5)
        sqr(5)
        rmul(5, "G")
        fis(6)
        fis(7)
        f_mul(1)
        mx(4, 3)
        stt(4, 3)
        f_sum(1)
        q_int(0, 0, H)
        q_int(0, H, H)
        for k in range(5, 8):
            mx(k, 3)
            stt(k, 3)
        fchi(4, "S")
        st(6)
        for i in range(2, 6):
            t_kern(i)
            c_kern(i, "S")
            if i == 2:
                fchi(5, "S")
                fchi(6, "S")
            if i == 4:
                fchi(7, "S")
        inv(6)
        for i in range(6, 8):
            t_kern(i)
            c_kern(i, "S")
        st(7)
        inv(7)
        rmul(7, "G")
        q_kern(0, 0)
        q_kern(0, 1)
        q_int(1, 0, H)
        q_q(0, 0, G)
        q_q(1, 0, H)
        q_int(1, H, H)
        rmul(6, "V")
        q_q(1, H, H)
        q_kern(1, 0)
        q_kern(1, 1)
        for g, c0 in ((0, 0), (1, 0), (0, H)):
            for b0 in (c0, c0 + P):
                tr(g, b0)
                out(g, b0)
            store(g, c0, H)
            r_int(g, c0, H, "S")
        tr(1, H)
        out(1, H)
        store(1, H, P)
        q_r(0, 0, H)
        store_w(0, 0, H)
        tr(1, H + P)
        out(1, H + P)
        store(1, H + P, P)
        r_int(1, H, P, "S")
        q_r(1, 0, H)
        store_w(1, 0, H)
        r_int(1, H + P, P, "V")
        q_r(0, H, H)
        store_w(0, H, H)
        q_r(1, H, P)
        q_r(1, H + P, P)
        for k in range(4):
            store_s(0, k, "S")
        store_w(1, H, P)
        store_w(1, H + P, P)
        for k in range(4):
            store_s(1, k, "S" if k % 2 else "Y")
